import numpy as np
CORES = [4,12,20,28,36,44,52,60,132,140,148,156,164,172,180,188]
N = 16
T = 128
ROUTE = [[[0,9],[12,5],[9,10],[15,4],[11,6],[14,9],[14,11],[2,1],[12,5],[2,15],[6,13],[7,15],[7,3],[6,5],[15,13],[5,4],[12,15],[9,14],[5,1],[1,10],[13,10],[2,12],[8,7],[5,2],[5,0],[5,4],[9,0],[3,10],[8,11],[7,13],[3,12],[14,10],[1,14],[5,2],[8,2],[6,8],[0,13],[9,4],[7,9],[0,14],[6,11],[15,7],[2,14],[1,9],[12,13],[14,12],[2,10],[10,13],[1,5],[3,14],[0,5],[8,11],[1,10],[14,1],[4,1],[15,6],[12,6],[12,8],[15,4],[1,12],[5,14],[14,11],[15,9],[3,14],[10,15],[4,2],[7,10],[1,2],[8,1],[3,1],[15,13],[11,9],[1,8],[6,9],[10,4],[14,7],[9,1],[2,13],[3,10],[10,13],[10,0],[2,3],[9,3],[9,1],[6,11],[8,12],[2,15],[5,0],[6,7],[11,6],[0,9],[15,8],[2,4],[14,4],[1,12],[10,8],[6,2],[11,5],[14,10],[10,4],[10,14],[5,10],[12,10],[4,5],[2,11],[5,7],[15,5],[3,2],[12,0],[5,14],[1,12],[5,14],[7,3],[9,6],[3,5],[15,0],[12,11],[8,15],[1,2],[12,13],[13,7],[4,13],[14,4],[7,1],[6,10],[13,6],[2,9],[8,5]],[[11,8],[0,6],[12,9],[0,14],[3,7],[6,15],[3,13],[7,4],[5,13],[7,0],[4,15],[12,9],[1,10],[4,13],[8,10],[0,14],[10,2],[5,0],[15,3],[9,1],[15,10],[15,9],[4,5],[9,10],[13,6],[9,0],[3,9],[12,6],[1,6],[8,5],[6,7],[14,15],[9,2],[4,15],[13,2],[4,7],[2,13],[3,0],[10,2],[11,2],[15,10],[9,12],[9,7],[3,12],[10,3],[14,6],[1,3],[7,6],[12,6],[6,2],[3,7],[5,13],[7,11],[6,1],[12,8],[9,7],[6,4],[14,8],[0,2],[8,13],[3,10],[5,8],[3,10],[11,13],[14,3],[6,7],[1,13],[1,7],[4,12],[13,15],[6,2],[4,5],[15,9],[14,2],[4,14],[11,14],[11,12],[14,0],[3,8],[10,2],[14,11],[13,11],[10,12],[5,1],[6,7],[11,12],[12,9],[13,6],[4,8],[13,3],[13,8],[4,5],[12,11],[12,5],[4,5],[7,11],[5,3],[1,8],[14,11],[15,3],[9,3],[7,12],[6,8],[15,7],[10,1],[9,5],[4,11],[3,0],[1,4],[11,12],[0,5],[2,10],[9,0],[10,9],[3,11],[14,7],[3,15],[14,7],[15,4],[0,3],[6,9],[5,12],[6,2],[5,13],[4,1],[15,2],[3,9],[0,2]],[[8,9],[5,1],[12,11],[11,6],[13,1],[2,8],[1,0],[0,6],[9,13],[3,0],[7,1],[15,1],[11,15],[9,4],[11,4],[9,2],[4,5],[15,1],[15,1],[14,10],[0,13],[12,5],[8,6],[4,0],[4,8],[7,15],[12,6],[6,2],[7,12],[14,8],[4,5],[14,1],[15,12],[4,5],[12,8],[10,4],[4,8],[12,6],[14,12],[0,8],[9,15],[5,14],[4,15],[5,15],[10,9],[9,11],[10,15],[8,12],[14,6],[9,4],[9,5],[2,3],[9,4],[13,10],[12,11],[4,0],[13,10],[7,14],[8,1],[14,13],[2,5],[7,3],[11,7],[14,13],[8,6],[9,12],[1,15],[2,14],[12,11],[6,8],[3,4],[6,9],[15,5],[6,7],[15,2],[1,14],[12,3],[9,3],[10,2],[11,13],[0,8],[9,13],[12,6],[11,1],[1,11],[3,9],[1,13],[10,4],[8,15],[4,10],[10,13],[7,9],[3,9],[11,10],[14,0],[12,8],[13,15],[14,1],[7,5],[7,15],[4,5],[4,8],[3,4],[9,13],[8,5],[9,0],[12,3],[1,11],[8,13],[1,5],[13,8],[4,9],[0,4],[15,12],[10,5],[1,15],[3,14],[2,15],[3,13],[0,6],[5,8],[12,15],[2,3],[7,12],[14,9],[5,11],[10,7],[11,6]],[[4,1],[3,6],[0,3],[1,7],[11,12],[10,9],[7,9],[4,15],[9,7],[8,6],[10,13],[1,0],[4,15],[4,9],[4,12],[3,10],[7,15],[0,12],[8,2],[0,12],[3,13],[10,8],[6,15],[11,9],[9,4],[11,13],[15,11],[12,0],[5,6],[6,7],[14,3],[13,5],[14,13],[0,12],[5,0],[0,13],[5,0],[15,5],[11,4],[8,1],[4,12],[10,0],[14,5],[14,5],[13,10],[11,10],[12,2],[9,1],[1,5],[14,5],[1,10],[0,14],[13,6],[5,12],[3,15],[11,3],[1,4],[1,0],[9,12],[11,0],[1,0],[6,3],[9,11],[5,12],[13,11],[5,6],[0,13],[12,8],[11,3],[11,13],[14,12],[1,15],[7,0],[15,9],[1,15],[12,7],[14,9],[7,15],[1,10],[0,7],[9,7],[4,13],[9,14],[7,6],[15,13],[10,13],[8,2],[15,9],[13,9],[15,8],[9,6],[3,13],[8,0],[9,6],[7,12],[6,10],[7,14],[10,6],[10,13],[3,15],[12,3],[13,15],[12,10],[5,1],[13,3],[7,12],[12,1],[1,0],[9,10],[13,7],[0,1],[11,14],[11,6],[14,9],[7,13],[15,7],[12,10],[12,0],[1,4],[12,5],[6,15],[4,2],[13,7],[14,0],[11,15],[10,1],[15,9],[9,11]],[[6,9],[10,5],[9,1],[3,11],[13,0],[7,3],[3,13],[4,11],[1,15],[13,2],[11,6],[5,2],[6,13],[4,1],[7,6],[14,12],[8,7],[13,8],[6,14],[10,8],[11,3],[12,8],[15,5],[9,12],[1,10],[11,14],[0,7],[6,11],[4,3],[10,6],[3,9],[2,7],[9,12],[0,4],[14,1],[7,6],[12,2],[0,9],[1,0],[13,2],[1,15],[8,11],[0,5],[7,1],[12,4],[1,7],[1,7],[11,1],[13,11],[12,1],[14,12],[5,4],[5,1],[4,8],[15,11],[4,9],[13,4],[7,15],[15,10],[13,1],[4,14],[2,0],[10,15],[6,14],[7,10],[2,15],[15,3],[12,10],[1,6],[2,3],[11,1],[3,9],[5,8],[2,12],[15,0],[0,5],[5,14],[2,5],[10,15],[11,0],[11,3],[7,10],[10,7],[7,12],[12,13],[12,11],[9,3],[12,9],[11,9],[3,2],[4,9],[13,2],[8,5],[13,3],[4,8],[6,0],[1,5],[13,0],[0,15],[2,0],[6,9],[10,13],[14,2],[14,8],[6,14],[8,10],[8,13],[15,10],[1,9],[12,2],[10,11],[13,0],[13,3],[5,8],[2,8],[1,0],[11,14],[0,1],[1,13],[2,12],[8,13],[11,4],[7,0],[3,12],[8,9],[4,0],[0,11],[6,12]],[[2,4],[2,6],[15,12],[2,9],[14,11],[4,3],[13,1],[2,12],[10,9],[4,7],[10,4],[2,9],[7,8],[7,15],[6,0],[11,2],[13,6],[15,0],[15,0],[12,0],[2,6],[10,14],[5,15],[5,2],[4,3],[12,15],[12,4],[4,5],[7,6],[12,5],[3,6],[11,1],[2,15],[13,4],[15,10],[1,14],[10,3],[15,4],[9,5],[8,11],[3,4],[3,6],[11,5],[8,2],[15,6],[1,9],[7,3],[14,12],[1,6],[12,10],[2,8],[5,13],[1,2],[8,10],[7,5],[7,1],[0,4],[3,14],[9,2],[10,12],[6,12],[14,6],[11,1],[10,0],[14,0],[4,10],[3,15],[15,11],[10,11],[4,8],[11,14],[0,4],[10,3],[6,11],[15,5],[12,8],[14,3],[8,13],[11,13],[0,8],[9,1],[8,1],[8,6],[7,10],[0,15],[4,3],[4,15],[10,0],[8,5],[15,9],[14,4],[0,3],[0,15],[10,0],[13,14],[7,5],[1,2],[9,10],[13,14],[10,11],[0,15],[6,14],[11,6],[13,15],[15,7],[5,12],[13,7],[8,11],[13,10],[7,8],[2,8],[8,0],[12,10],[13,8],[2,12],[13,12],[13,4],[0,8],[13,3],[5,2],[9,3],[13,14],[13,2],[13,1],[1,14],[12,10],[13,12],[4,13]],[[12,11],[3,8],[3,9],[5,12],[13,5],[1,7],[1,13],[14,3],[4,10],[13,11],[10,11],[5,7],[0,5],[1,3],[1,6],[6,12],[1,2],[14,4],[10,2],[5,14],[1,4],[14,15],[15,12],[11,10],[8,9],[6,15],[8,2],[10,4],[7,2],[11,12],[9,13],[1,6],[10,12],[5,12],[6,13],[9,15],[0,9],[1,11],[3,1],[14,2],[2,3],[8,1],[8,3],[12,2],[13,5],[1,3],[2,12],[3,5],[8,11],[15,12],[11,3],[14,7],[14,4],[13,15],[3,9],[8,2],[11,8],[12,5],[5,2],[2,14],[0,15],[5,2],[11,4],[9,15],[11,4],[1,7],[9,5],[11,10],[13,10],[14,6],[12,9],[3,10],[14,8],[0,5],[0,6],[12,0],[6,9],[10,0],[9,15],[0,9],[11,10],[13,14],[4,14],[4,12],[9,13],[1,5],[8,7],[10,15],[13,2],[8,7],[6,7],[0,15],[0,12],[13,0],[2,0],[7,9],[6,2],[10,4],[9,7],[11,3],[5,12],[3,7],[13,8],[9,10],[13,5],[1,2],[9,4],[1,3],[6,5],[3,11],[4,6],[11,14],[5,13],[15,12],[0,6],[0,8],[4,3],[3,8],[13,9],[15,8],[4,5],[5,14],[1,12],[5,13],[2,14],[9,3],[3,11],[0,14]],[[8,13],[13,12],[2,5],[6,4],[4,6],[12,3],[12,3],[5,8],[5,10],[8,15],[6,8],[12,8],[10,4],[9,11],[4,7],[9,0],[8,14],[2,3],[0,1],[13,11],[9,0],[15,9],[0,7],[4,6],[1,0],[15,6],[3,7],[11,8],[12,11],[2,7],[7,10],[8,9],[8,0],[3,5],[0,14],[14,12],[4,3],[1,10],[10,4],[2,3],[15,13],[11,12],[12,8],[7,15],[7,1],[11,8],[14,15],[15,4],[6,8],[1,8],[8,11],[7,0],[1,8],[2,8],[0,9],[11,14],[5,13],[14,8],[10,4],[0,12],[12,11],[3,10],[5,7],[7,0],[8,15],[11,6],[8,6],[5,9],[12,3],[6,8],[14,8],[10,4],[8,4],[8,13],[2,13],[13,1],[1,9],[10,11],[11,8],[6,10],[2,9],[6,12],[4,3],[0,4],[13,4],[12,0],[8,11],[10,1],[5,10],[7,9],[6,14],[14,13],[8,1],[7,15],[6,12],[11,12],[14,13],[13,0],[0,6],[10,1],[8,3],[8,9],[12,4],[15,5],[15,0],[13,15],[2,13],[15,13],[13,0],[8,0],[10,9],[12,8],[13,0],[2,12],[3,10],[13,6],[5,10],[3,1],[8,7],[11,15],[1,9],[12,7],[15,5],[1,8],[13,6],[15,6],[7,15],[12,5]],[[11,15],[5,3],[8,15],[6,5],[15,4],[2,7],[0,9],[12,9],[7,14],[15,14],[3,9],[8,4],[4,11],[2,7],[10,4],[2,6],[9,13],[2,11],[13,14],[8,9],[6,15],[13,6],[15,6],[1,9],[4,9],[7,4],[5,10],[4,7],[14,9],[4,11],[8,12],[7,10],[0,4],[7,4],[2,11],[8,2],[10,3],[10,14],[7,2],[9,12],[5,9],[10,7],[11,2],[11,2],[9,10],[14,6],[1,15],[9,7],[12,13],[1,8],[11,15],[7,3],[2,5],[5,12],[0,5],[14,11],[5,11],[13,15],[9,8],[14,11],[1,0],[15,2],[9,10],[11,1],[6,7],[13,7],[2,12],[12,15],[6,1],[15,14],[3,6],[11,6],[7,12],[7,1],[12,14],[15,11],[7,1],[13,7],[9,11],[0,15],[14,11],[4,5],[11,15],[3,14],[13,2],[12,1],[9,13],[0,3],[15,11],[11,6],[9,4],[13,5],[3,15],[15,7],[5,4],[7,13],[2,6],[10,1],[10,15],[1,12],[14,7],[10,7],[13,7],[4,10],[14,13],[4,6],[5,3],[10,8],[3,15],[7,14],[1,9],[13,7],[1,10],[5,6],[2,14],[10,6],[6,9],[7,4],[9,0],[2,11],[2,3],[4,15],[14,5],[5,1],[5,9],[8,9],[15,14],[15,13]],[[8,1],[2,3],[12,15],[3,0],[3,13],[6,1],[4,0],[14,9],[12,14],[14,11],[2,12],[7,15],[8,14],[12,9],[0,12],[10,15],[10,9],[15,3],[8,10],[2,0],[10,6],[15,11],[0,14],[5,12],[0,2],[13,12],[1,3],[1,5],[6,5],[1,9],[11,15],[8,15],[12,3],[12,14],[13,7],[10,5],[14,6],[7,8],[8,11],[7,12],[9,0],[4,0],[11,0],[12,6],[4,11],[0,14],[4,5],[13,10],[14,6],[6,15],[5,0],[12,15],[4,6],[0,5],[9,1],[14,2],[14,7],[13,1],[13,11],[9,1],[10,6],[12,8],[1,15],[6,12],[9,2],[3,14],[8,1],[9,3],[4,3],[3,9],[15,3],[2,5],[7,1],[10,5],[3,1],[14,4],[5,2],[10,2],[15,2],[10,0],[5,15],[12,0],[5,13],[2,10],[12,15],[14,0],[0,5],[6,10],[12,7],[3,13],[14,15],[11,4],[1,7],[11,4],[4,14],[15,7],[4,3],[0,13],[2,14],[13,6],[8,2],[2,10],[11,9],[4,8],[7,1],[15,9],[12,3],[8,13],[12,2],[10,6],[7,5],[4,12],[2,11],[1,12],[6,2],[3,14],[1,13],[14,6],[3,8],[6,5],[13,14],[0,9],[6,10],[9,4],[12,15],[11,1],[7,6],[14,6]],[[1,12],[13,4],[14,8],[9,15],[6,9],[0,15],[9,11],[12,3],[14,2],[11,12],[10,5],[9,3],[1,3],[13,6],[15,8],[14,11],[15,4],[4,2],[11,10],[12,2],[9,12],[11,0],[13,1],[12,11],[5,3],[1,13],[10,12],[6,0],[8,14],[8,14],[14,15],[3,15],[12,3],[11,2],[4,14],[2,1],[3,5],[11,2],[10,3],[10,14],[5,8],[14,5],[9,10],[4,7],[10,14],[14,1],[6,10],[0,7],[11,1],[13,8],[0,11],[15,8],[9,12],[13,14],[2,0],[11,6],[8,1],[6,9],[7,13],[6,0],[3,6],[9,8],[6,8],[14,0],[11,2],[1,10],[12,1],[5,8],[0,7],[6,11],[2,0],[1,7],[14,3],[9,6],[8,15],[1,7],[2,15],[4,8],[4,11],[13,12],[4,5],[6,10],[4,14],[9,15],[4,7],[14,13],[2,9],[4,14],[5,14],[1,3],[3,10],[1,13],[0,8],[3,10],[14,0],[2,7],[2,0],[6,15],[8,13],[12,3],[15,7],[4,8],[11,13],[1,5],[9,4],[13,15],[13,8],[3,8],[10,0],[0,8],[6,12],[0,10],[3,9],[14,3],[7,0],[2,1],[12,5],[14,1],[4,1],[10,3],[3,2],[15,8],[3,10],[10,8],[8,14],[11,10],[5,9],[11,8]],[[7,10],[1,0],[13,1],[14,10],[12,15],[14,8],[13,14],[0,9],[8,15],[0,2],[7,9],[11,10],[14,4],[14,6],[0,6],[1,6],[12,15],[10,13],[10,2],[3,12],[6,9],[0,15],[13,2],[1,12],[10,11],[0,4],[13,0],[7,3],[14,0],[9,0],[7,11],[11,8],[11,8],[5,11],[13,7],[5,8],[3,7],[3,11],[4,1],[15,11],[14,9],[9,7],[0,11],[12,10],[6,4],[7,1],[2,8],[13,8],[1,4],[9,12],[12,4],[4,1],[12,15],[5,12],[4,6],[0,15],[14,13],[9,4],[9,6],[14,15],[4,12],[14,13],[14,7],[1,2],[9,3],[2,3],[2,6],[7,9],[4,8],[6,12],[11,2],[13,14],[14,4],[15,6],[11,6],[15,5],[0,4],[11,13],[8,3],[15,13],[15,9],[1,3],[7,3],[13,7],[3,1],[7,0],[6,11],[0,11],[11,6],[8,10],[13,10],[12,0],[6,1],[5,0],[0,8],[10,3],[3,5],[3,5],[4,8],[9,6],[13,4],[1,14],[3,14],[15,11],[5,8],[11,4],[6,14],[8,6],[9,8],[6,14],[7,1],[13,14],[8,13],[0,11],[1,13],[12,7],[8,9],[9,12],[2,4],[3,8],[12,15],[14,5],[9,7],[13,1],[13,0],[7,4],[12,6],[4,2]],[[4,9],[2,8],[11,15],[3,9],[1,2],[7,14],[9,14],[0,5],[4,11],[5,11],[7,2],[13,3],[6,8],[13,15],[4,7],[13,11],[0,7],[5,8],[7,2],[12,11],[12,15],[7,3],[13,15],[7,10],[15,9],[6,5],[0,11],[11,2],[1,0],[7,12],[10,1],[12,14],[14,11],[4,10],[7,6],[2,11],[15,7],[3,9],[2,13],[12,13],[0,7],[5,1],[8,14],[10,8],[12,3],[7,15],[2,6],[13,0],[12,15],[9,0],[3,7],[10,4],[9,8],[7,12],[2,12],[0,10],[6,4],[14,10],[14,5],[14,5],[7,12],[3,4],[4,6],[8,1],[6,13],[7,2],[5,8],[15,3],[4,7],[8,4],[12,5],[10,4],[3,14],[11,9],[12,0],[6,8],[3,13],[9,5],[13,2],[15,12],[10,12],[4,8],[6,9],[2,10],[9,10],[3,0],[13,7],[4,12],[6,12],[10,11],[9,8],[3,12],[3,7],[6,5],[2,13],[3,5],[4,15],[5,12],[4,6],[14,3],[10,6],[15,2],[12,7],[15,8],[5,15],[3,12],[13,2],[8,5],[4,1],[11,10],[6,3],[6,0],[6,1],[2,5],[1,5],[6,12],[11,5],[5,3],[13,9],[15,10],[3,9],[3,6],[14,3],[4,12],[10,8],[13,8],[9,14],[2,7]],[[0,9],[15,1],[2,4],[11,10],[11,4],[2,10],[1,3],[6,14],[7,3],[2,10],[5,10],[6,5],[5,1],[8,13],[9,13],[11,12],[13,11],[15,14],[2,8],[15,9],[11,4],[13,14],[5,8],[13,11],[4,8],[4,1],[6,9],[5,1],[13,11],[10,14],[11,1],[13,7],[4,6],[3,12],[12,5],[6,15],[1,10],[0,2],[6,9],[10,0],[3,5],[7,3],[14,7],[5,1],[5,3],[14,10],[0,11],[10,2],[13,0],[1,15],[2,3],[13,9],[9,3],[9,15],[5,15],[6,7],[13,11],[7,10],[15,9],[7,13],[0,11],[4,5],[2,3],[10,6],[8,7],[1,11],[0,2],[3,0],[5,13],[10,3],[13,1],[8,12],[9,13],[0,5],[11,7],[13,9],[12,7],[9,2],[11,10],[15,2],[10,12],[0,4],[10,13],[14,3],[6,15],[10,6],[15,6],[11,3],[15,13],[1,7],[14,5],[4,14],[10,0],[4,0],[4,7],[7,10],[8,6],[9,2],[8,5],[14,13],[8,2],[12,1],[10,8],[0,5],[0,13],[12,15],[10,15],[6,9],[9,13],[3,0],[0,9],[3,8],[1,12],[3,2],[0,2],[6,13],[13,12],[4,10],[11,10],[6,5],[8,5],[7,14],[8,0],[7,1],[0,8],[7,11],[0,1],[5,8]],[[15,1],[2,11],[8,6],[6,14],[2,6],[8,7],[12,7],[3,9],[12,0],[1,13],[9,0],[5,0],[9,8],[3,8],[4,13],[15,4],[5,8],[9,3],[11,14],[2,7],[1,10],[13,2],[6,1],[2,13],[1,10],[9,6],[3,11],[13,9],[13,4],[3,14],[5,10],[2,7],[9,0],[5,8],[10,15],[7,11],[13,0],[1,8],[2,7],[13,3],[3,7],[4,11],[8,1],[3,5],[0,2],[8,4],[15,5],[2,11],[0,5],[3,5],[8,14],[7,13],[7,10],[13,7],[3,4],[4,13],[12,9],[11,1],[6,4],[11,13],[2,4],[4,6],[10,15],[4,15],[2,6],[2,8],[8,12],[7,14],[5,1],[15,10],[12,2],[7,8],[3,12],[4,3],[3,2],[1,9],[7,2],[0,13],[13,7],[11,12],[6,8],[1,9],[15,7],[15,8],[11,2],[9,5],[14,13],[7,3],[12,9],[14,0],[14,1],[10,0],[6,2],[9,3],[2,8],[6,10],[10,5],[11,8],[0,5],[4,2],[1,9],[14,0],[2,11],[4,3],[6,7],[0,14],[15,14],[5,13],[11,2],[12,8],[1,9],[12,13],[1,2],[9,14],[4,2],[10,8],[9,10],[9,2],[4,13],[7,5],[9,1],[8,0],[7,6],[15,13],[10,8],[14,3],[15,13],[13,5]],[[2,1],[6,1],[8,9],[11,8],[1,6],[10,0],[4,10],[15,6],[5,2],[6,12],[10,6],[8,15],[1,8],[0,14],[2,14],[14,15],[7,14],[0,12],[10,2],[5,10],[8,1],[15,5],[1,13],[12,13],[8,11],[3,1],[7,12],[8,0],[9,12],[7,8],[12,10],[11,8],[14,9],[2,8],[2,5],[13,2],[14,4],[3,2],[7,1],[10,2],[3,7],[2,8],[1,15],[3,8],[6,9],[2,6],[5,7],[13,12],[13,8],[0,8],[2,4],[12,8],[0,3],[8,9],[1,15],[11,9],[2,6],[1,6],[13,15],[0,1],[9,8],[11,13],[8,12],[15,12],[9,15],[15,8],[11,0],[14,9],[7,12],[1,5],[4,6],[14,15],[8,9],[15,6],[1,3],[12,15],[7,5],[14,1],[13,14],[5,12],[1,5],[0,8],[6,13],[5,1],[13,11],[14,7],[11,0],[6,11],[9,13],[0,6],[8,11],[4,7],[11,7],[0,7],[6,3],[12,3],[0,12],[4,0],[0,2],[7,14],[1,0],[6,3],[12,14],[13,15],[3,9],[14,4],[6,1],[9,1],[13,12],[11,13],[8,15],[11,14],[2,0],[13,6],[13,1],[11,12],[12,9],[12,5],[11,1],[7,12],[0,14],[9,14],[11,7],[12,5],[2,6],[6,14],[6,13],[11,3]]]
ZW = 280
def setup_inputs(rng):
    return {"z": rng.standard_normal((N, 128, ZW), dtype=np.float32)}
def reference(z):
    y = np.zeros((N, 128, T), np.float64)
    fill = [0] * N
    for r in range(N):
        for t in range(T):
            for e in ROUTE[r][t]:
                y[r][:, t] += z[e][:, fill[e]].astype(np.float64)
                fill[e] += 1
    return {"y": y.astype(z.dtype)}

@@ -1,0 +1,103 @@
+from concourse.bass import DstId, RemoteDMATransfer
+
+N = 16
+LW = 402
+
+SCRATCH = {
+    "zs": ("sbuf", [128, 280], "float32"),
+    "land": ("sbuf", [128, LW], "float32"),
+    "F": ("sbuf", [128, 128], "float32"),
+}
+SEMAPHORES = ["ld", "sent", "arr1", "arr2", "farr", "st"]
+
+
+def plan(route):
+    cnt = [[0] * N for _ in range(N)]
+    for r in range(N):
+        for pair in route[r]:
+            for e in pair:
+                cnt[e][r] += 1
+    off = [[sum(cnt[e][:r]) for r in range(N + 1)] for e in range(N)]
+    fill = [0] * N
+    col = [[None] * len(route[r]) for r in range(N)]
+    for r in range(N):
+        for t, pair in enumerate(route[r]):
+            c = []
+            for e in pair:
+                c.append((e, fill[e]))
+                fill[e] += 1
+            col[r][t] = c
+    base = [[0] * N for _ in range(N)]
+    for c in range(N):
+        p = 0
+        for e in range(N):
+            if e % 2 == c % 2:
+                base[c][e] = p
+                p += cnt[e][c & ~1] + cnt[e][c | 1]
+        for e in range(N):
+            if e % 2 != c % 2:
+                base[c][e] = p
+                p += cnt[e][c]
+        assert p <= LW, p
+    return cnt, off, col, base
+
+
+def rank_program(g, core, T, topo):
+    route = T.tables["ROUTE"]
+    cores = T.cores
+    cnt, off, col, base = plan(route)
+    rank = T.rank_of(core)
+    S = T.sem
+    if rank is not None:
+        e = rank
+        tot = off[e][N]
+        g.dma_start(T.zs[:, 0:tot], T.z[:, 0:tot]).then_inc(S.ld, 16)
+        g.wait_ge(S.ld, 16)
+        sent = 0
+        for c in range(N):
+            if c % 2 != e % 2:
+                continue
+            d = cores[c] + 2
+            rid, pid = topo.addr(d, core)
+            m = topo.mask(core, d)
+            a, b = off[e][c & ~1], off[e][(c | 1) + 1]
+            g.remote_dma(T.land[:, base[c][e]:base[c][e] + b - a], T.zs[:, a:b], S.arr1, S.sent, pid, rid, m)
+            sent += 16 if m == 0xFFFF else 8
+        g.wait_ge(S.farr, 128)
+        g.dma_start(T.y[:, :], T.F[:, :]).then_inc(S.st, 16)
+        g.wait_ge(S.st, 16)
+        g.wait_ge(S.sent, sent)
+        return
+    c = T.rank_of(core - 2)
+    if c is None:
+        return
+    mate = c ^ 1
+    g.wait_ge(S.arr1, 7 * 8 + 16)
+    d = cores[mate] + 2
+    rid, pid = topo.addr(d, core)
+    sent = 0
+    for e in range(N):
+        if e % 2 != c % 2:
+            continue
+        s0 = base[c][e] + off[e][mate] - off[e][c & ~1]
+        w = cnt[e][mate]
+        g.remote_dma(T.land[:, base[mate][e]:base[mate][e] + w], T.land[:, s0:s0 + w], S.arr2, S.sent, pid, rid, 0xFF)
+        sent += 8
+    g.wait_ge(S.arr2, 64)
+    rid, pid = topo.addr(cores[c], core)
+    for t0 in range(0, 128, 16):
+        trs = []
+        for i in range(16):
+            t = t0 + i
+            srcs = []
+            for (e, k) in col[c][t]:
+                if e % 2 == c % 2:
+                    p = base[c][e] + k - off[e][c & ~1]
+                else:
+                    p = base[c][e] + k - off[e][c]
+                srcs.append(T.land[:, p:p + 1])
+            trs.append(RemoteDMATransfer(dst_ids=[DstId(rid=rid, pnc=pid)], dma_engine_mask=1 << i, remote_sem=S.farr,
+                                         srcs=srcs, dsts=[T.F[:, t:t + 1]], alu_op=1))
+            sent += 1
+        g.remote_dma_fused(trs, local_sem=S.sent)
+    g.wait_ge(S.sent, sent)

@@ -1,103 +1,210 @@
 from concourse.bass import DstId, RemoteDMATransfer
+from concourse.mybir import AluOpType
 
 N = 16
-LW = 402
+NT = 128
+ZW = 280
 
 SCRATCH = {
-    "zs": ("sbuf", [128, 280], "float32"),
-    "land": ("sbuf", [128, LW], "float32"),
-    "F": ("sbuf", [128, 128], "float32"),
+    "zs": ("sbuf", [128, ZW], "float32"),
+    "F0": ("sbuf", [128, NT], "float32"),
+    "F1": ("sbuf", [128, NT], "float32"),
 }
-SEMAPHORES = ["ld", "sent", "arr1", "arr2", "farr", "st"]
+SEMAPHORES = ["ld", "got", "sent", "a0", "a1", "st0", "st1"]
+
+CORE4_EXTRA = 20
+CACHE = {}
+
+
+def choose_dies(cnt, nit):
+    def cost(die):
+        load = {}
+        for e in range(N):
+            load[(3, e, 0)], load[(3, e, 1)] = CORE4_EXTRA, 0
+            for r in range(N):
+                d, v = die[e][r], cnt[e][r]
+                load[(3, e, d)] += nit[e][r]
+                if r == e:
+                    continue
+                if (e ^ r) & 1:
+                    keys = [(0, e, d)] + ([(1, e ^ 1, d), (2, r, d)] if r != e ^ 1 else [])
+                else:
+                    keys = [(1, e, d), (2, r, d)]
+                for k in keys:
+                    load[k] = load.get(k, 0) + v
+        return sum((v * (4 if k[0] == 0 else 1 if k[0] == 3 else 2)) ** 4 for k, v in load.items())
+
+    die = [[((e >> 1) + (r >> 1)) & 1 for r in range(N)] for e in range(N)]
+    best = cost(die)
+    better = True
+    while better:
+        better = False
+        for e in range(N):
+            for r in range(N):
+                die[e][r] ^= 1
+                c = cost(die)
+                if c < best:
+                    best, better = c, True
+                else:
+                    die[e][r] ^= 1
+    return die
+
+
+def cut(items, shares):
+    tot = float(sum(shares))
+    out, a, acc = [], 0, 0.0
+    for s in shares:
+        acc += s
+        b = int(round(len(items) * acc / tot)) if tot > 0 else len(items)
+        out.append(items[a:b])
+        a = b
+    return out
+
+
+def share_out(cross, same, d, e):
+    port = (6, 7) if d == 0 else (2, 3)
+    extra = CORE4_EXTRA if d == 0 else 0
+    fair = (len(cross) + len(same) + extra) / 4.0
+    w = {}
+    w[port[0]], w[port[1]] = cut(cross, [1, 1])
+    left = list(same)
+    for c in port:
+        mine = w[c]
+        grown = True
+        while grown and len(mine) + 1 <= fair:
+            grown = False
+            ends = set(it[0] + it[1] for it in mine)
+            starts = set(it[0] for it in mine)
+            for it in left:
+                if it[0] in ends or it[0] + it[1] in starts:
+                    mine.append(it)
+                    left.remove(it)
+                    grown = True
+                    break
+        mine.sort()
+    if d == 0:
+        h = (len(left) + extra) / 2.0
+        own = [it for it in left if it[2] == e]
+        rest = [it for it in left if it[2] != e]
+        a, b = cut(rest, [max(h - len(own), 0.0), max(h - extra, 0.0)])
+        w[5], w[4] = sorted(a + own), b
+    else:
+        w[0], w[1] = cut(left, [1, 1])
+    return w
+
+
+def make_calls(items, e):
+    calls = []
+    for onchip in (False, True):
+        for w in sorted(set(it[1] for it in items)):
+            grp = [it for it in items if it[1] == w and (it[2] == e) == onchip]
+            for i in range(0, len(grp), 8):
+                part = grp[i:i + 8]
+                p = 8
+                while p * len(part) > 8:
+                    p //= 2
+                lo = 8 if onchip else 0
+                calls.append([(it, ((1 << p) - 1) << (lo + j * p), p) for j, it in enumerate(part)])
+    return calls
 
 
 def plan(route):
+    if "p" in CACHE:
+        return CACHE["p"]
     cnt = [[0] * N for _ in range(N)]
-    for r in range(N):
-        for pair in route[r]:
-            for e in pair:
-                cnt[e][r] += 1
-    off = [[sum(cnt[e][:r]) for r in range(N + 1)] for e in range(N)]
     fill = [0] * N
-    col = [[None] * len(route[r]) for r in range(N)]
+    blocks = [[[] for _ in range(N)] for _ in range(N)]
     for r in range(N):
+        first = 0
         for t, pair in enumerate(route[r]):
-            c = []
-            for e in pair:
-                c.append((e, fill[e]))
+            if t > 0:
+                prev = route[r][t - 1]
+                for k in (0, 1):
+                    if pair[k] in prev:
+                        first = (first ^ prev.index(pair[k])) ^ k
+                        break
+            for k, e in enumerate(pair):
+                s = first ^ k
+                b = blocks[e][r]
+                if b and b[-1][0] + b[-1][1] == fill[e] and b[-1][3] + b[-1][1] == t and b[-1][4] == s:
+                    b[-1] = (b[-1][0], b[-1][1] + 1, r, b[-1][3], s)
+                else:
+                    b.append((fill[e], 1, r, t, s))
                 fill[e] += 1
-            col[r][t] = c
-    base = [[0] * N for _ in range(N)]
-    for c in range(N):
-        p = 0
-        for e in range(N):
-            if e % 2 == c % 2:
-                base[c][e] = p
-                p += cnt[e][c & ~1] + cnt[e][c | 1]
-        for e in range(N):
-            if e % 2 != c % 2:
-                base[c][e] = p
-                p += cnt[e][c]
-        assert p <= LW, p
-    return cnt, off, col, base
+                cnt[e][r] += 1
+    die = choose_dies(cnt, [[len(blocks[e][r]) for r in range(N)] for e in range(N)])
+    work = []
+    need = [[0, 0] for _ in range(N)]
+    for e in range(N):
+        w = {}
+        for d in (0, 1):
+            cross = [it for r in range(N) if (r ^ e) & 1 and die[e][r] == d for it in blocks[e][r]]
+            same = [it for r in range(N) if not (r ^ e) & 1 and die[e][r] == d for it in blocks[e][r]]
+            w.update(share_out(cross, same, d, e))
+        we = {}
+        for c, items in w.items():
+            pieces = []
+            for it in items:
+                if pieces and pieces[-1][1] == it[0]:
+                    pieces[-1][1] = it[0] + it[1]
+                else:
+                    pieces.append([it[0], it[0] + it[1]])
+            calls = make_calls(items, e)
+            for call in calls:
+                for it, m, p in call:
+                    need[it[2]][it[4]] += p
+            we[c] = (pieces, calls)
+        work.append(we)
+    CACHE["p"] = {"tot": fill, "work": work, "need": need, "die": die, "cnt": cnt}
+    return CACHE["p"]
+
+
+def send_columns(g, core, T, topo, calls):
+    sent = 0
+    for call in calls:
+        trs = []
+        for (k, w, r, t, s), m, p in call:
+            rid, pid = topo.addr(T.cores[r], core)
+            trs.append(RemoteDMATransfer(dst_ids=[DstId(rid=rid, pnc=pid)], dma_engine_mask=m,
+                                         remote_sem=T.sem["a%d" % s], src=T.zs[:, k:k + w],
+                                         dst=T["F%d" % s][:, t:t + w]))
+            sent += p
+        g.remote_dma_fused(trs, local_sem=T.sem.sent)
+    return sent
 
 
 def rank_program(g, core, T, topo):
-    route = T.tables["ROUTE"]
-    cores = T.cores
-    cnt, off, col, base = plan(route)
-    rank = T.rank_of(core)
+    e = T.rank_of(core - core % 8 + 4)
+    if e is None:
+        return
+    P = plan(T.tables["ROUTE"])
     S = T.sem
-    if rank is not None:
-        e = rank
-        tot = off[e][N]
-        g.dma_start(T.zs[:, 0:tot], T.z[:, 0:tot]).then_inc(S.ld, 16)
-        g.wait_ge(S.ld, 16)
-        sent = 0
-        for c in range(N):
-            if c % 2 != e % 2:
-                continue
-            d = cores[c] + 2
-            rid, pid = topo.addr(d, core)
-            m = topo.mask(core, d)
-            a, b = off[e][c & ~1], off[e][(c | 1) + 1]
-            g.remote_dma(T.land[:, base[c][e]:base[c][e] + b - a], T.zs[:, a:b], S.arr1, S.sent, pid, rid, m)
-            sent += 16 if m == 0xFFFF else 8
-        g.wait_ge(S.farr, 128)
-        g.dma_start(T.y[:, :], T.F[:, :]).then_inc(S.st, 16)
-        g.wait_ge(S.st, 16)
+    work = P["work"][e]
+    pieces, calls = work[core % 8]
+
+    if core % 8 != 4:
+        if not pieces:
+            return
+        g.wait_ge(S.got, 16 * len(pieces))
+        sent = send_columns(g, core, T, topo, calls)
         g.wait_ge(S.sent, sent)
         return
-    c = T.rank_of(core - 2)
-    if c is None:
-        return
-    mate = c ^ 1
-    g.wait_ge(S.arr1, 7 * 8 + 16)
-    d = cores[mate] + 2
-    rid, pid = topo.addr(d, core)
+
+    g.sync.dma_start(T.zs[:, 0:P["tot"][e]], T.z[:, 0:P["tot"][e]]).then_inc(S.ld, 16)
+    g.wait_ge(S.ld, 16)
     sent = 0
-    for e in range(N):
-        if e % 2 != c % 2:
-            continue
-        s0 = base[c][e] + off[e][mate] - off[e][c & ~1]
-        w = cnt[e][mate]
-        g.remote_dma(T.land[:, base[mate][e]:base[mate][e] + w], T.land[:, s0:s0 + w], S.arr2, S.sent, pid, rid, 0xFF)
-        sent += 8
-    g.wait_ge(S.arr2, 64)
-    rid, pid = topo.addr(cores[c], core)
-    for t0 in range(0, 128, 16):
-        trs = []
-        for i in range(16):
-            t = t0 + i
-            srcs = []
-            for (e, k) in col[c][t]:
-                if e % 2 == c % 2:
-                    p = base[c][e] + k - off[e][c & ~1]
-                else:
-                    p = base[c][e] + k - off[e][c]
-                srcs.append(T.land[:, p:p + 1])
-            trs.append(RemoteDMATransfer(dst_ids=[DstId(rid=rid, pnc=pid)], dma_engine_mask=1 << i, remote_sem=S.farr,
-                                         srcs=srcs, dsts=[T.F[:, t:t + 1]], alu_op=1))
-            sent += 1
-        g.remote_dma_fused(trs, local_sem=S.sent)
+    for c in (6, 2, 7, 3, 5, 0, 1):
+        d = core - 4 + c
+        rid, pid = topo.addr(d, core)
+        for a, b in work[c][0]:
+            g.remote_dma(T.zs[:, a:b], T.zs[:, a:b], S.got, S.sent, pid, rid, 0xFFFF)
+            sent += 16
+    sent += send_columns(g, core, T, topo, calls)
+    need = P["need"][e]
+    g.sync.wait_ge(S.a0, need[0])
+    g.sync.dma_start(T.y[:, :], T.F0[:, :]).then_inc(S.st0, 16)
+    g.wait_ge(S.a1, need[1])
+    g.wait_ge(S.st0, 16)
+    g.dma_start(T.y[:, :], T.F1[:, :], accum_op=AluOpType.add).then_inc(S.st1, 16)
     g.wait_ge(S.sent, sent)
+    g.wait_ge(S.st1, 16)

@@ -12,7 +12,7 @@ SCRATCH = {
 }
 SEMAPHORES = ["ld", "got", "sent", "a0", "a1", "st0", "st1"]
 
-CORE4_EXTRA = 20
+CORE4_EXTRA = 21
 CACHE = {}
 
 
@@ -32,7 +32,7 @@ def choose_dies(cnt, nit):
                     keys = [(1, e, d), (2, r, d)]
                 for k in keys:
                     load[k] = load.get(k, 0) + v
-        return sum((v * (4 if k[0] == 0 else 1 if k[0] == 3 else 2)) ** 4 for k, v in load.items())
+        return sum((v * (9 if k[0] == 0 else 4 if k[0] == 3 else 5)) ** 4 for k, v in load.items())
 
     die = [[((e >> 1) + (r >> 1)) & 1 for r in range(N)] for e in range(N)]
     best = cost(die)
@@ -81,6 +81,9 @@ def share_out(cross, same, d, e):
                     left.remove(it)
                     grown = True
                     break
+            if not grown and left:
+                mine.append(left.pop(0))
+                grown = True
         mine.sort()
     if d == 0:
         h = (len(left) + extra) / 2.0

from concourse.bass import DstId, RemoteDMATransfer
from concourse.mybir import AluOpType

N = 16
NT = 128
ZW = 280

SCRATCH = {
    "zs": ("sbuf", [128, ZW], "float32"),
    "F0": ("sbuf", [128, NT], "float32"),
    "F1": ("sbuf", [128, NT], "float32"),
}
SEMAPHORES = ["ld", "got", "sent", "a0", "a1", "st0", "st1"]

CORE4_EXTRA = 21
CACHE = {}


def choose_dies(cnt, nit):
    def cost(die):
        load = {}
        for e in range(N):
            load[(3, e, 0)], load[(3, e, 1)] = CORE4_EXTRA, 0
            for r in range(N):
                d, v = die[e][r], cnt[e][r]
                load[(3, e, d)] += nit[e][r]
                if r == e:
                    continue
                if (e ^ r) & 1:
                    keys = [(0, e, d)] + ([(1, e ^ 1, d), (2, r, d)] if r != e ^ 1 else [])
                else:
                    keys = [(1, e, d), (2, r, d)]
                for k in keys:
                    load[k] = load.get(k, 0) + v
        return sum((v * (9 if k[0] == 0 else 4 if k[0] == 3 else 5)) ** 4 for k, v in load.items())

    die = [[((e >> 1) + (r >> 1)) & 1 for r in range(N)] for e in range(N)]
    best = cost(die)
    better = True
    while better:
        better = False
        for e in range(N):
            for r in range(N):
                die[e][r] ^= 1
                c = cost(die)
                if c < best:
                    best, better = c, True
                else:
                    die[e][r] ^= 1
    return die


def cut(items, shares):
    tot = float(sum(shares))
    out, a, acc = [], 0, 0.0
    for s in shares:
        acc += s
        b = int(round(len(items) * acc / tot)) if tot > 0 else len(items)
        out.append(items[a:b])
        a = b
    return out


def share_out(cross, same, d, e):
    port = (6, 7) if d == 0 else (2, 3)
    extra = CORE4_EXTRA if d == 0 else 0
    fair = (len(cross) + len(same) + extra) / 4.0
    w = {}
    w[port[0]], w[port[1]] = cut(cross, [1, 1])
    left = list(same)
    for c in port:
        mine = w[c]
        grown = True
        while grown and len(mine) + 1 <= fair:
            grown = False
            ends = set(it[0] + it[1] for it in mine)
            starts = set(it[0] for it in mine)
            for it in left:
                if it[0] in ends or it[0] + it[1] in starts:
                    mine.append(it)
                    left.remove(it)
                    grown = True
                    break
            if not grown and left:
                mine.append(left.pop(0))
                grown = True
        mine.sort()
    if d == 0:
        h = (len(left) + extra) / 2.0
        own = [it for it in left if it[2] == e]
        rest = [it for it in left if it[2] != e]
        a, b = cut(rest, [max(h - len(own), 0.0), max(h - extra, 0.0)])
        w[5], w[4] = sorted(a + own), b
    else:
        w[0], w[1] = cut(left, [1, 1])
    return w


def make_calls(items, e):
    calls = []
    for onchip in (False, True):
        for w in sorted(set(it[1] for it in items)):
            grp = [it for it in items if it[1] == w and (it[2] == e) == onchip]
            for i in range(0, len(grp), 8):
                part = grp[i:i + 8]
                p = 8
                while p * len(part) > 8:
                    p //= 2
                lo = 8 if onchip else 0
                calls.append([(it, ((1 << p) - 1) << (lo + j * p), p) for j, it in enumerate(part)])
    return calls


def plan(route):
    if "p" in CACHE:
        return CACHE["p"]
    cnt = [[0] * N for _ in range(N)]
    fill = [0] * N
    blocks = [[[] for _ in range(N)] for _ in range(N)]
    for r in range(N):
        first = 0
        for t, pair in enumerate(route[r]):
            if t > 0:
                prev = route[r][t - 1]
                for k in (0, 1):
                    if pair[k] in prev:
                        first = (first ^ prev.index(pair[k])) ^ k
                        break
            for k, e in enumerate(pair):
                s = first ^ k
                b = blocks[e][r]
                if b and b[-1][0] + b[-1][1] == fill[e] and b[-1][3] + b[-1][1] == t and b[-1][4] == s:
                    b[-1] = (b[-1][0], b[-1][1] + 1, r, b[-1][3], s)
                else:
                    b.append((fill[e], 1, r, t, s))
                fill[e] += 1
                cnt[e][r] += 1
    die = choose_dies(cnt, [[len(blocks[e][r]) for r in range(N)] for e in range(N)])
    work = []
    need = [[0, 0] for _ in range(N)]
    for e in range(N):
        w = {}
        for d in (0, 1):
            cross = [it for r in range(N) if (r ^ e) & 1 and die[e][r] == d for it in blocks[e][r]]
            same = [it for r in range(N) if not (r ^ e) & 1 and die[e][r] == d for it in blocks[e][r]]
            w.update(share_out(cross, same, d, e))
        we = {}
        for c, items in w.items():
            pieces = []
            for it in items:
                if pieces and pieces[-1][1] == it[0]:
                    pieces[-1][1] = it[0] + it[1]
                else:
                    pieces.append([it[0], it[0] + it[1]])
            calls = make_calls(items, e)
            for call in calls:
                for it, m, p in call:
                    need[it[2]][it[4]] += p
            we[c] = (pieces, calls)
        work.append(we)
    CACHE["p"] = {"tot": fill, "work": work, "need": need, "die": die, "cnt": cnt}
    return CACHE["p"]


def send_columns(g, core, T, topo, calls):
    sent = 0
    for call in calls:
        trs = []
        for (k, w, r, t, s), m, p in call:
            rid, pid = topo.addr(T.cores[r], core)
            trs.append(RemoteDMATransfer(dst_ids=[DstId(rid=rid, pnc=pid)], dma_engine_mask=m,
                                         remote_sem=T.sem["a%d" % s], src=T.zs[:, k:k + w],
                                         dst=T["F%d" % s][:, t:t + w]))
            sent += p
        g.remote_dma_fused(trs, local_sem=T.sem.sent)
    return sent


def rank_program(g, core, T, topo):
    e = T.rank_of(core - core % 8 + 4)
    if e is None:
        return
    P = plan(T.tables["ROUTE"])
    S = T.sem
    work = P["work"][e]
    pieces, calls = work[core % 8]

    if core % 8 != 4:
        if not pieces:
            return
        g.wait_ge(S.got, 16 * len(pieces))
        sent = send_columns(g, core, T, topo, calls)
        g.wait_ge(S.sent, sent)
        return

    g.sync.dma_start(T.zs[:, 0:P["tot"][e]], T.z[:, 0:P["tot"][e]]).then_inc(S.ld, 16)
    g.wait_ge(S.ld, 16)
    sent = 0
    for c in (6, 2, 7, 3, 5, 0, 1):
        d = core - 4 + c
        rid, pid = topo.addr(d, core)
        for a, b in work[c][0]:
            g.remote_dma(T.zs[:, a:b], T.zs[:, a:b], S.got, S.sent, pid, rid, 0xFFFF)
            sent += 16
    sent += send_columns(g, core, T, topo, calls)
    need = P["need"][e]
    g.sync.wait_ge(S.a0, need[0])
    g.sync.dma_start(T.y[:, :], T.F0[:, :]).then_inc(S.st0, 16)
    g.wait_ge(S.a1, need[1])
    g.wait_ge(S.st0, 16)
    g.dma_start(T.y[:, :], T.F1[:, :], accum_op=AluOpType.add).then_inc(S.st1, 16)
    g.wait_ge(S.sent, sent)
    g.wait_ge(S.st1, 16)
